import numpy as np
import ml_dtypes


def mxq(x, axis, fmt="e4m3"):
    dtype, down = {"e4m3": (ml_dtypes.float8_e4m3fn, 7), "e5m2": (ml_dtypes.float8_e5m2, 14)}[fmt]
    v = np.moveaxis(np.asarray(x, np.float32).astype(ml_dtypes.bfloat16).astype(np.float64), axis, -1)
    blocks = v.reshape(v.shape[:-1] + (-1, 32))
    amax = np.abs(blocks).max(-1, keepdims=True)
    byte = np.maximum(np.where(amax > 0, np.frexp(amax)[1] - 1 + 127, 0) - down, 1)
    scale = np.exp2(byte - 127.0)
    codes = (blocks / scale).astype(np.float32).astype(dtype).astype(np.float64)
    return np.moveaxis((codes * scale).reshape(v.shape), -1, axis)


WIDE = False


def mx_kscale(k):
    if not WIDE:
        return np.ones(k)
    levels = np.array([10, -10, 5, -5, 0])
    if k % 512:
        return np.exp2(np.random.permutation(np.resize(levels, k // 32))).repeat(32)
    a = np.empty((k // 512, 16))
    for p in range(k // 512):
        a[p, :8] = np.random.permutation(np.resize(levels, 8))
        for g in range(8):
            far = levels[np.abs(levels - a[p, g]) >= 10]
            a[p, g + 8] = far[np.random.randint(len(far))]
    return np.exp2(a.ravel()).repeat(32)


def f64(x):
    return np.asarray(x).astype(np.float64)


def striped(idx):
    return np.tile(idx.reshape(-1, 16).T, (8, 1)).astype(np.uint16)


def unstriped(offs):
    return offs[:16].T.reshape(-1).astype(np.int64)


def pack_weight(w):
    k, n = w.shape
    w = f64(np.asarray(w, np.float32).astype(ml_dtypes.bfloat16)).reshape(k // 32, 32, n)
    amax = np.abs(w).max(1)
    byte = np.clip(np.where(amax > 0, np.frexp(amax)[1] - 1 + 127 - 7, 1), 1, 254)
    scaled = (w * np.exp2(127.0 - byte)[:, None, :]).reshape(k, n).astype(np.float32)
    words = np.ascontiguousarray(scaled.reshape(k // 512, 128, 4, n).transpose(0, 1, 3, 2)).astype(ml_dtypes.float8_e4m3fn).view(np.uint8)
    return words, np.ascontiguousarray(byte.astype(np.uint8).reshape(k // 512, 16, n))


def unpack_weight(words, scales):
    g, p, n, _ = words.shape
    vals = np.ascontiguousarray(words).view(ml_dtypes.float8_e4m3fn).astype(np.float64) * np.repeat(np.exp2(scales.astype(np.float64) - 127.0), 8, axis=1)[..., None]
    return vals.transpose(0, 1, 3, 2).reshape(g * 512, n)


def relu(v):
    return np.maximum(v, 0.0)


K, T, S, D, N = 512, 2048, 1024, 4, 128
P = 2 ** 7


def setup_inputs():
    n = np.random.standard_normal
    s = mx_kscale(K)[:, None]
    packed_xT = pack_weight(n((K, T)) * s)
    return {
        "x_words": packed_xT[0],
        "x_scales": packed_xT[1],
        "w1": (n((K, N)) / np.sqrt(K) / s).astype(np.float32),
        "w2": (n((K, N)) / np.sqrt(K) / s).astype(np.float32),
        "rad": (np.random.uniform(0.8, 1.6, (N, 1))).astype(np.float32),
        "stif": (np.tile(np.random.uniform(0.8, 1.6, S), (P, 1))).astype(np.float32),
        "offs": striped(np.random.permutation(T)[:S]),
    }


def reference(x_words, x_scales, w1, w2, rad, stif, offs):
    xq = unpack_weight(x_words, x_scales)[:, unstriped(offs)]
    yv = mxq(f64(w2), 0, "e4m3").T @ xq
    yn = mxq(f64(w1), 0, "e4m3").T @ xq
    over = relu(-1.0 * np.abs(yn) + f64(rad))
    fn = (over * np.sqrt(over + 0.01)) * f64(stif)[:1]
    ft = np.maximum(np.minimum(0.5 * yv, 0.6 * fn), -0.6 * fn)
    fc = ft + (fn * yn) / (np.abs(yn) + 0.1)
    return fc.reshape(len(fc), -1, D).sum(axis=2)

@@ -1,0 +1,200 @@
+from contextlib import ExitStack
+
+import concourse.mybir as mybir
+from concourse.masks import make_identity
+
+K, T, S, D, N = 512, 2048, 1024, 4, 128
+FLOPS = 2 * 2 * K * N * S
+
+F32 = mybir.dt.float32
+BF16 = mybir.dt.bfloat16
+I32 = mybir.dt.int32
+U32 = mybir.dt.uint32
+U16 = mybir.dt.uint16
+U8 = mybir.dt.uint8
+FP8X4 = mybir.dt.float8_e4m3fn_x4
+ALU = mybir.AluOpType
+ACT = mybir.ActivationFunctionType
+
+P = 128
+PACK = 4
+BLOCK = P * D
+HALF = BLOCK // 2
+
+
+def tile_picked_ydem_force_p_kernel(tc, x_words, x_scales, w1, w2, rad, stif, offs, out):
+    nc = tc.nc
+    with ExitStack() as ctx:
+        keep = ctx.enter_context(tc.tile_pool(name="keep", bufs=1))
+        psum = ctx.enter_context(tc.psum_pool(name="psum", bufs=1))
+
+        offsets = keep.tile([P, S // 16], U16, name="offsets")
+        nc.sync.dma_start(offsets[:], offs)
+        w1_raw = keep.tile([P, PACK, N], F32, name="w1_raw")
+        nc.sync.dma_start(w1_raw[:], w1.rearrange("(p j) m -> p j m", j=PACK))
+
+        scale_table = keep.tile([P, T], U8, name="scale_table", align_bytes=64)
+        nc.vector.memset(scale_table[:].bitcast(I32), 0)
+        for q in range(4):
+            nc.sync.dma_start(
+                scale_table[32 * q : 32 * q + 4, :].bitcast(I32),
+                x_scales[0, 4 * q : 4 * q + 4, :].bitcast(I32),
+            )
+
+        w2_raw = keep.tile([P, PACK, N], F32, name="w2_raw")
+        nc.sync.dma_start(w2_raw[:], w2.rearrange("(p j) m -> p j m", j=PACK))
+        word_table = keep.tile([P, T], U32, name="word_table", align_bytes=64)
+        nc.sync.dma_start(word_table[:].bitcast(I32), x_words[0].rearrange("p n t -> p (n t)").bitcast(I32))
+        rad_col = keep.tile([P, 1], F32, name="rad_col")
+        nc.sync.dma_start(rad_col[:], rad)
+
+        stif_cols = keep.tile([P, 2, D], F32, name="stif_cols")
+        nc.gpsimd.dma_start(stif_cols[:], stif[0:1, :].rearrange("o (b n d) -> n (o b) d", n=P, d=D))
+        ident = keep.tile([P, P], F32, name="ident")
+        make_identity(nc, ident[:])
+
+        def gather(table, dtype, start, width, name):
+            picked = keep.tile([P, width], dtype, name="%s%d" % (name, start), align_bytes=64)
+            nc.vector.tensor_copy(picked[:], table[:].indirect(offsets[:, start // 16 : (start + width) // 16]))
+            return picked
+
+        def quantise(raw, name):
+            grouped = keep.tile([P, N, PACK], BF16, name=name + "_grouped", align_bytes=64)
+            nc.scalar.copy(
+                grouped[:].rearrange("p (c i) j -> p c j i", i=4), raw[:].rearrange("p j (c i) -> p c j i", i=4)
+            )
+            codes = keep.tile([P, N], U32, name=name + "_codes", align_bytes=64)
+            scales = keep.tile([P, N], U8, name=name + "_scales", align_bytes=64)
+            nc.vector.quantize_mx(codes[:].bitcast(FP8X4), scales[:], grouped[:].rearrange("p m j -> p (m j)"))
+            return codes, scales
+
+        x_scales_picked = gather(scale_table, U8, 0, S, "scales")
+        w1_mx = quantise(w1_raw, "w1")
+        w2_mx = quantise(w2_raw, "w2")
+
+        stif_banks = []
+        for b in range(2):
+            bank = psum.tile([P, D, P], F32, name="stif_bank%d" % b)
+            for d in range(D):
+                nc.tensor.transpose(bank[:, d, :], stif_cols[:, b, d : d + 1].to_broadcast([P, P]), ident[:])
+            stif_banks.append(bank)
+
+        def product(bank, weights, start, width, words):
+            nc.tensor.matmul_mx(
+                bank,
+                lhsT=weights[0][:].bitcast(FP8X4),
+                lhsT_scale=weights[1][:],
+                rhs=words[:].bitcast(FP8X4),
+                rhs_scale=x_scales_picked[:, start : start + width],
+                start=True,
+                stop=True,
+            )
+
+        tangential = [keep.tile([P, D, P], F32, name="tangential%d" % b) for b in range(2)]
+        normal = [keep.tile([P, D, P], F32, name="normal%d" % b) for b in range(2)]
+
+        units = []
+        for h in range(2):
+            words = gather(word_table, U32, h * HALF, HALF, "words")
+            bank = psum.tile([P, 2, HALF], F32, name="y_bank%d" % h)
+            product(bank[:, 0, :], w1_mx, h * HALF, HALF, words)
+            product(bank[:, 1, :], w2_mx, h * HALF, HALF, words)
+            grains = slice(h * P // 2, (h + 1) * P // 2)
+            units.append(
+                (
+                    bank[:, 0, :].rearrange("p (v d) -> p d v", d=D),
+                    bank[:, 1, :].rearrange("p (v d) -> p d v", d=D),
+                    stif_banks[0][:, :, grains],
+                    tangential[0][:, :, grains],
+                    normal[0][:, :, grains],
+                )
+            )
+        words = gather(word_table, U32, BLOCK, BLOCK, "words")
+        yn_bank = psum.tile([P, BLOCK], F32, name="yn_bank")
+        yv_bank = psum.tile([P, BLOCK], F32, name="yv_bank")
+        product(yn_bank[:], w1_mx, BLOCK, BLOCK, words)
+        product(yv_bank[:], w2_mx, BLOCK, BLOCK, words)
+        for h in range(2):
+            pair = slice(2 * h, 2 * h + 2)
+            units.append(
+                (
+                    yn_bank[:].rearrange("p (v d) -> p d v", d=D)[:, pair, :],
+                    yv_bank[:].rearrange("p (v d) -> p d v", d=D)[:, pair, :],
+                    stif_banks[1][:, pair, :],
+                    tangential[1][:, pair, :],
+                    normal[1][:, pair, :],
+                )
+            )
+
+        def fresh(name, u):
+            return keep.tile(list(units[u][0].shape), F32, name="%s%d" % (name, u))
+
+        def gap_of(u):
+            gap = keep.tile(list(units[u][0].shape), F32, name="gap")
+            nc.scalar.activation(gap[:], units[u][0], ACT.Abs)
+            return gap
+
+        made = []
+        gap = gap_of(0)
+        for u in range(len(units)):
+            over, root, shifted, soft, inverse = [fresh(n, u) for n in ("over", "root", "shifted", "soft", "inverse")]
+            nc.scalar.activation(over[:], gap[:], ACT.Relu, bias=rad_col[:], scale=-1.0)
+            nc.scalar.activation(soft[:], gap[:], ACT.Abs_reciprocal_sqrt, bias=0.1)
+            nc.scalar.activation(root[:], over[:], ACT.Abs_reciprocal_sqrt, bias=0.01)
+            nc.scalar.activation(shifted[:], over[:], ACT.Square, bias=0.005)
+            if u + 1 < len(units):
+                gap = gap_of(u + 1)
+            nc.scalar.activation(inverse[:], soft[:], ACT.Square)
+            made.append((root, shifted, inverse))
+
+        sums = [psum.tile([P, 2, P], F32, name="sums%d" % b) for b in range(2)]
+
+        def add_terms(b, members):
+            for term in (normal[b], tangential[b]):
+                for d in members:
+                    nc.tensor.matmul(
+                        sums[b][:, 0, :],
+                        term[:, d, :],
+                        ident[:],
+                        start=(d == 0 and term is normal[b]),
+                        stop=(d == D - 1 and term is tangential[b]),
+                        is_transpose=True,
+                    )
+
+        def hertz_of(u):
+            hertz = fresh("hertz", u)
+            root, shifted = made[u][:2]
+            nc.vector.scalar_tensor_tensor(hertz[:], shifted[:], 0.005 * 0.005, root[:], ALU.subtract, ALU.mult)
+            return hertz
+
+        hertz = hertz_of(0)
+        for u, (yn, yv, stiff, tang, norm) in enumerate(units):
+            inverse = made[u][2]
+            cap, upper, slope = [fresh(n, u) for n in ("cap", "upper", "slope")]
+            nc.vector.scalar_tensor_tensor(cap[:], hertz[:], 0.6, stiff, ALU.mult, ALU.mult)
+            nc.vector.scalar_tensor_tensor(slope[:], yn, 1.0 / 0.6, inverse[:], ALU.mult, ALU.mult)
+            nc.vector.scalar_tensor_tensor(upper[:], yv, 0.5, cap[:], ALU.mult, ALU.min)
+            nc.vector.tensor_tensor(norm, cap[:], slope[:], ALU.mult)
+            if u + 1 < len(units):
+                hertz = hertz_of(u + 1)
+            nc.vector.scalar_tensor_tensor(tang, cap[:], -1.0, upper[:], ALU.mult, ALU.max)
+            if u == 1:
+                add_terms(0, range(D))
+                turned = keep.tile([P, P], F32, name="turned0")
+                nc.scalar.copy(turned[:], sums[0][:, 0, :])
+                nc.tensor.transpose(sums[0][:, 1, :], turned[:], ident[:])
+                result = keep.tile([P, P], F32, name="result0")
+                nc.scalar.copy(result[:], sums[0][:, 1, :])
+                nc.sync.dma_start(out[:, 0:P], result[:])
+            if u >= 2:
+                add_terms(1, range(2 * (u - 2), 2 * (u - 1)))
+
+        turned = keep.tile([P, P], F32, name="turned1", align_bytes=64)
+        nc.vector.transpose(turned[:], sums[1][:, 0, :])
+        rows = out.rearrange("(g i) v -> i g v", i=32)
+        for a in range(4):
+            queue = nc.sync if a % 2 == 0 else nc.scalar
+            queue.dma_start(
+                rows[:, :, P + 32 * a : P + 32 * (a + 1)],
+                turned[32 * a : 32 * (a + 1), :].rearrange("p (g j) -> p g j", j=32),
+            )

@@ -20,6 +20,7 @@ P = 128
 PACK = 4
 BLOCK = P * D
 HALF = BLOCK // 2
+FIRST = 768
 
 
 def tile_picked_ydem_force_p_kernel(tc, x_words, x_scales, w1, w2, rad, stif, offs, out):
@@ -32,6 +33,9 @@ def tile_picked_ydem_force_p_kernel(tc, x_words, x_scales, w1, w2, rad, stif, of
         nc.sync.dma_start(offsets[:], offs)
         w1_raw = keep.tile([P, PACK, N], F32, name="w1_raw")
         nc.sync.dma_start(w1_raw[:], w1.rearrange("(p j) m -> p j m", j=PACK))
+        word_table = keep.tile([P, T], U32, name="word_table", align_bytes=64)
+        x_rows = x_words[0].rearrange("p n t -> p (n t)").bitcast(I32)
+        nc.sync.dma_start(word_table[:, :FIRST].bitcast(I32), x_rows[:, :FIRST])
 
         scale_table = keep.tile([P, T], U8, name="scale_table", align_bytes=64)
         nc.vector.memset(scale_table[:].bitcast(I32), 0)
@@ -41,20 +45,23 @@ def tile_picked_ydem_force_p_kernel(tc, x_words, x_scales, w1, w2, rad, stif, of
                 x_scales[0, 4 * q : 4 * q + 4, :].bitcast(I32),
             )
 
-        w2_raw = keep.tile([P, PACK, N], F32, name="w2_raw")
+        nc.sync.dma_start(word_table[:, FIRST:].bitcast(I32), x_rows[:, FIRST:])
+        w2_raw = keep.tile([P, PACK, N], F32, name="w2_raw", align_bytes=64)
         nc.sync.dma_start(w2_raw[:], w2.rearrange("(p j) m -> p j m", j=PACK))
-        word_table = keep.tile([P, T], U32, name="word_table", align_bytes=64)
-        nc.sync.dma_start(word_table[:].bitcast(I32), x_words[0].rearrange("p n t -> p (n t)").bitcast(I32))
         rad_col = keep.tile([P, 1], F32, name="rad_col")
         nc.sync.dma_start(rad_col[:], rad)
 
         stif_cols = keep.tile([P, 2, D], F32, name="stif_cols")
-        nc.gpsimd.dma_start(stif_cols[:], stif[0:1, :].rearrange("o (b n d) -> n (o b) d", n=P, d=D))
+        nc.sync.dma_start(stif_cols[:], stif[0:1, :].rearrange("o (b n d) -> n (o b) d", n=P, d=D))
+        seed = keep.tile([P, 1], F32, name="seed")
+        nc.gpsimd.memset(seed[:], 1.0)
+        warm = keep.tile([P, 1], F32, name="warm")
+        nc.scalar.activation(warm[:], seed[:], ACT.Abs_reciprocal_sqrt, bias=0.1)
         ident = keep.tile([P, P], F32, name="ident")
         make_identity(nc, ident[:])
 
-        def gather(table, dtype, start, width, name):
-            picked = keep.tile([P, width], dtype, name="%s%d" % (name, start), align_bytes=64)
+        def gather(table, dtype, start, width, name, tag=""):
+            picked = keep.tile([P, width], dtype, name="%s%d" % (name, start), tag=tag, align_bytes=64)
             nc.vector.tensor_copy(picked[:], table[:].indirect(offsets[:, start // 16 : (start + width) // 16]))
             return picked
 
@@ -68,52 +75,56 @@ def tile_picked_ydem_force_p_kernel(tc, x_words, x_scales, w1, w2, rad, stif, of
             nc.vector.quantize_mx(codes[:].bitcast(FP8X4), scales[:], grouped[:].rearrange("p m j -> p (m j)"))
             return codes, scales
 
-        x_scales_picked = gather(scale_table, U8, 0, S, "scales")
+        early_scales = gather(scale_table, U8, 0, BLOCK, "scales")
         w1_mx = quantise(w1_raw, "w1")
         w2_mx = quantise(w2_raw, "w2")
 
-        stif_banks = []
-        for b in range(2):
-            bank = psum.tile([P, D, P], F32, name="stif_bank%d" % b)
-            for d in range(D):
-                nc.tensor.transpose(bank[:, d, :], stif_cols[:, b, d : d + 1].to_broadcast([P, P]), ident[:])
-            stif_banks.append(bank)
+        stif_banks = [psum.tile([P, D, P], F32, name="stif_bank%d" % b) for b in range(2)]
 
-        def product(bank, weights, start, width, words):
+        def product(bank, weights, words, scales):
             nc.tensor.matmul_mx(
                 bank,
                 lhsT=weights[0][:].bitcast(FP8X4),
                 lhsT_scale=weights[1][:],
-                rhs=words[:].bitcast(FP8X4),
-                rhs_scale=x_scales_picked[:, start : start + width],
+                rhs=words.bitcast(FP8X4),
+                rhs_scale=scales,
                 start=True,
                 stop=True,
             )
 
-        tangential = [keep.tile([P, D, P], F32, name="tangential%d" % b) for b in range(2)]
+        tangential = keep.tile([P, D, P], F32, name="tangential")
         normal = [keep.tile([P, D, P], F32, name="normal%d" % b) for b in range(2)]
 
+        def spread_stiffness(b):
+            for d in range(D):
+                nc.tensor.transpose(stif_banks[b][:, d, :], stif_cols[:, b, d : d + 1].to_broadcast([P, P]), ident[:])
+
         units = []
+        early_words = []
+        yv_halves = psum.tile([P, 2, HALF], F32, name="yv_halves")
         for h in range(2):
-            words = gather(word_table, U32, h * HALF, HALF, "words")
-            bank = psum.tile([P, 2, HALF], F32, name="y_bank%d" % h)
-            product(bank[:, 0, :], w1_mx, h * HALF, HALF, words)
-            product(bank[:, 1, :], w2_mx, h * HALF, HALF, words)
+            early_words.append(gather(word_table, U32, h * HALF, HALF, "words"))
+            yn_half = psum.tile([P, HALF], F32, name="yn_half%d" % h)
+            product(yn_half[:], w1_mx, early_words[h][:], early_scales[:, h * HALF : (h + 1) * HALF])
             grains = slice(h * P // 2, (h + 1) * P // 2)
             units.append(
                 (
-                    bank[:, 0, :].rearrange("p (v d) -> p d v", d=D),
-                    bank[:, 1, :].rearrange("p (v d) -> p d v", d=D),
+                    yn_half[:].rearrange("p (v d) -> p d v", d=D),
+                    yv_halves[:, h, :].rearrange("p (v d) -> p d v", d=D),
                     stif_banks[0][:, :, grains],
-                    tangential[0][:, :, grains],
-                    normal[0][:, :, grains],
+                    (slice(None), slice(None), grains),
                 )
             )
-        words = gather(word_table, U32, BLOCK, BLOCK, "words")
+        spread_stiffness(0)
+        for h in range(2):
+            product(yv_halves[:, h, :], w2_mx, early_words[h][:], early_scales[:, h * HALF : (h + 1) * HALF])
+        late_words = gather(word_table, U32, BLOCK, BLOCK, "words")
+        late_scales = gather(scale_table, U8, BLOCK, BLOCK, "scales", tag="w2_raw")
         yn_bank = psum.tile([P, BLOCK], F32, name="yn_bank")
         yv_bank = psum.tile([P, BLOCK], F32, name="yv_bank")
-        product(yn_bank[:], w1_mx, BLOCK, BLOCK, words)
-        product(yv_bank[:], w2_mx, BLOCK, BLOCK, words)
+        product(yn_bank[:], w1_mx, late_words[:], late_scales[:])
+        product(yv_bank[:], w2_mx, late_words[:], late_scales[:])
+        spread_stiffness(1)
         for h in range(2):
             pair = slice(2 * h, 2 * h + 2)
             units.append(
@@ -121,8 +132,7 @@ def tile_picked_ydem_force_p_kernel(tc, x_words, x_scales, w1, w2, rad, stif, of
                     yn_bank[:].rearrange("p (v d) -> p d v", d=D)[:, pair, :],
                     yv_bank[:].rearrange("p (v d) -> p d v", d=D)[:, pair, :],
                     stif_banks[1][:, pair, :],
-                    tangential[1][:, pair, :],
-                    normal[1][:, pair, :],
+                    (slice(None), pair, slice(None)),
                 )
             )
 
@@ -139,27 +149,27 @@ def tile_picked_ydem_force_p_kernel(tc, x_words, x_scales, w1, w2, rad, stif, of
         for u in range(len(units)):
             over, root, shifted, soft, inverse = [fresh(n, u) for n in ("over", "root", "shifted", "soft", "inverse")]
             nc.scalar.activation(over[:], gap[:], ACT.Relu, bias=rad_col[:], scale=-1.0)
-            nc.scalar.activation(soft[:], gap[:], ACT.Abs_reciprocal_sqrt, bias=0.1)
+            if u > 0:
+                nc.scalar.activation(soft[:], gap[:], ACT.Abs_reciprocal_sqrt, bias=0.1)
             nc.scalar.activation(root[:], over[:], ACT.Abs_reciprocal_sqrt, bias=0.01)
             nc.scalar.activation(shifted[:], over[:], ACT.Square, bias=0.005)
+            if u == 0:
+                nc.scalar.activation(soft[:], gap[:], ACT.Abs_reciprocal_sqrt, bias=0.1)
             if u + 1 < len(units):
                 gap = gap_of(u + 1)
             nc.scalar.activation(inverse[:], soft[:], ACT.Square)
             made.append((root, shifted, inverse))
 
-        sums = [psum.tile([P, 2, P], F32, name="sums%d" % b) for b in range(2)]
-
-        def add_terms(b, members):
-            for term in (normal[b], tangential[b]):
-                for d in members:
-                    nc.tensor.matmul(
-                        sums[b][:, 0, :],
-                        term[:, d, :],
-                        ident[:],
-                        start=(d == 0 and term is normal[b]),
-                        stop=(d == D - 1 and term is tangential[b]),
-                        is_transpose=True,
-                    )
+        def add_turned(bank, terms, first=True, last=True):
+            for i, term in enumerate(terms):
+                nc.tensor.matmul(
+                    bank,
+                    term,
+                    ident[:],
+                    start=(first and i == 0),
+                    stop=(last and i == len(terms) - 1),
+                    is_transpose=True,
+                )
 
         def hertz_of(u):
             hertz = fresh("hertz", u)
@@ -167,30 +177,43 @@ def tile_picked_ydem_force_p_kernel(tc, x_words, x_scales, w1, w2, rad, stif, of
             nc.vector.scalar_tensor_tensor(hertz[:], shifted[:], 0.005 * 0.005, root[:], ALU.subtract, ALU.mult)
             return hertz
 
+        caps = [keep.tile([P, D, P], F32, name="cap%d" % b) for b in range(2)]
+        uppers = [keep.tile([P, D, P], F32, name="upper%d" % b) for b in range(2)]
         hertz = hertz_of(0)
-        for u, (yn, yv, stiff, tang, norm) in enumerate(units):
+        for u, (yn, yv, stiff, part) in enumerate(units):
+            b = u // 2
             inverse = made[u][2]
-            cap, upper, slope = [fresh(n, u) for n in ("cap", "upper", "slope")]
-            nc.vector.scalar_tensor_tensor(cap[:], hertz[:], 0.6, stiff, ALU.mult, ALU.mult)
+            cap, upper, slope = caps[b][part], uppers[b][part], fresh("slope", u)
+            nc.vector.scalar_tensor_tensor(cap, hertz[:], 0.6, stiff, ALU.mult, ALU.mult)
             nc.vector.scalar_tensor_tensor(slope[:], yn, 1.0 / 0.6, inverse[:], ALU.mult, ALU.mult)
-            nc.vector.scalar_tensor_tensor(upper[:], yv, 0.5, cap[:], ALU.mult, ALU.min)
-            nc.vector.tensor_tensor(norm, cap[:], slope[:], ALU.mult)
+            nc.vector.scalar_tensor_tensor(upper, yv, 0.5, cap, ALU.mult, ALU.min)
+            nc.vector.tensor_tensor(normal[b][part], slope[:], cap, ALU.mult)
             if u + 1 < len(units):
                 hertz = hertz_of(u + 1)
-            nc.vector.scalar_tensor_tensor(tang, cap[:], -1.0, upper[:], ALU.mult, ALU.max)
+            if b == 1:
+                nc.vector.scalar_tensor_tensor(tangential[part], cap, -1.0, upper, ALU.mult, ALU.max)
+                if u == 2:
+                    late_sums = psum.tile([P, P], F32, name="late_sums", tag="stif_bank0")
+                members = (2 * (u - 2), 2 * (u - 2) + 1)
+                terms = [term[:, d, :] for term in (normal[1], tangential) for d in members]
+                add_turned(late_sums[:], terms, first=(u == 2), last=(u == 3))
             if u == 1:
-                add_terms(0, range(D))
+                lifted = psum.tile([P, D, P], F32, name="lifted", tag="yn_half0")
+                for d in range(D):
+                    add_turned(lifted[:, d, :], [uppers[0][:, d, :], caps[0][:, d, :]])
+                early_sums = psum.tile([P, 2, P], F32, name="early_sums")
+                add_turned(early_sums[:, 0, :], [term[:, d, :] for term in (uppers[0], normal[0]) for d in range(D)])
+                clipped = keep.tile([P, D, P], F32, name="clipped")
+                nc.scalar.activation(clipped[:], lifted[:], ACT.Relu, scale=-1.0)
                 turned = keep.tile([P, P], F32, name="turned0")
-                nc.scalar.copy(turned[:], sums[0][:, 0, :])
-                nc.tensor.transpose(sums[0][:, 1, :], turned[:], ident[:])
+                nc.scalar.copy(turned[:], early_sums[:, 0, :])
+                add_turned(early_sums[:, 1, :], [turned[:]] + [clipped[:, d, :] for d in range(D)])
                 result = keep.tile([P, P], F32, name="result0")
-                nc.scalar.copy(result[:], sums[0][:, 1, :])
+                nc.scalar.copy(result[:], early_sums[:, 1, :])
                 nc.sync.dma_start(out[:, 0:P], result[:])
-            if u >= 2:
-                add_terms(1, range(2 * (u - 2), 2 * (u - 1)))
 
         turned = keep.tile([P, P], F32, name="turned1", align_bytes=64)
-        nc.vector.transpose(turned[:], sums[1][:, 0, :])
+        nc.vector.transpose(turned[:], late_sums[:])
         rows = out.rearrange("(g i) v -> i g v", i=32)
         for a in range(4):
             queue = nc.sync if a % 2 == 0 else nc.scalar

from contextlib import ExitStack

import concourse.mybir as mybir
from concourse.masks import make_identity

K, T, S, D, N = 512, 2048, 1024, 4, 128
FLOPS = 2 * 2 * K * N * S

F32 = mybir.dt.float32
BF16 = mybir.dt.bfloat16
I32 = mybir.dt.int32
U32 = mybir.dt.uint32
U16 = mybir.dt.uint16
U8 = mybir.dt.uint8
FP8X4 = mybir.dt.float8_e4m3fn_x4
ALU = mybir.AluOpType
ACT = mybir.ActivationFunctionType

P = 128
PACK = 4
BLOCK = P * D
HALF = BLOCK // 2
FIRST = 768


def tile_picked_ydem_force_p_kernel(tc, x_words, x_scales, w1, w2, rad, stif, offs, out):
    nc = tc.nc
    with ExitStack() as ctx:
        keep = ctx.enter_context(tc.tile_pool(name="keep", bufs=1))
        psum = ctx.enter_context(tc.psum_pool(name="psum", bufs=1))

        offsets = keep.tile([P, S // 16], U16, name="offsets")
        nc.sync.dma_start(offsets[:], offs)
        w1_raw = keep.tile([P, PACK, N], F32, name="w1_raw")
        nc.sync.dma_start(w1_raw[:], w1.rearrange("(p j) m -> p j m", j=PACK))
        word_table = keep.tile([P, T], U32, name="word_table", align_bytes=64)
        x_rows = x_words[0].rearrange("p n t -> p (n t)").bitcast(I32)
        nc.sync.dma_start(word_table[:, :FIRST].bitcast(I32), x_rows[:, :FIRST])

        scale_table = keep.tile([P, T], U8, name="scale_table", align_bytes=64)
        nc.vector.memset(scale_table[:].bitcast(I32), 0)
        for q in range(4):
            nc.sync.dma_start(
                scale_table[32 * q : 32 * q + 4, :].bitcast(I32),
                x_scales[0, 4 * q : 4 * q + 4, :].bitcast(I32),
            )

        nc.sync.dma_start(word_table[:, FIRST:].bitcast(I32), x_rows[:, FIRST:])
        w2_raw = keep.tile([P, PACK, N], F32, name="w2_raw", align_bytes=64)
        nc.sync.dma_start(w2_raw[:], w2.rearrange("(p j) m -> p j m", j=PACK))
        rad_col = keep.tile([P, 1], F32, name="rad_col")
        nc.sync.dma_start(rad_col[:], rad)

        stif_cols = keep.tile([P, 2, D], F32, name="stif_cols")
        nc.sync.dma_start(stif_cols[:], stif[0:1, :].rearrange("o (b n d) -> n (o b) d", n=P, d=D))
        seed = keep.tile([P, 1], F32, name="seed")
        nc.gpsimd.memset(seed[:], 1.0)
        warm = keep.tile([P, 1], F32, name="warm")
        nc.scalar.activation(warm[:], seed[:], ACT.Abs_reciprocal_sqrt, bias=0.1)
        ident = keep.tile([P, P], F32, name="ident")
        make_identity(nc, ident[:])

        def gather(table, dtype, start, width, name, tag=""):
            picked = keep.tile([P, width], dtype, name="%s%d" % (name, start), tag=tag, align_bytes=64)
            nc.vector.tensor_copy(picked[:], table[:].indirect(offsets[:, start // 16 : (start + width) // 16]))
            return picked

        def quantise(raw, name):
            grouped = keep.tile([P, N, PACK], BF16, name=name + "_grouped", align_bytes=64)
            nc.scalar.copy(
                grouped[:].rearrange("p (c i) j -> p c j i", i=4), raw[:].rearrange("p j (c i) -> p c j i", i=4)
            )
            codes = keep.tile([P, N], U32, name=name + "_codes", align_bytes=64)
            scales = keep.tile([P, N], U8, name=name + "_scales", align_bytes=64)
            nc.vector.quantize_mx(codes[:].bitcast(FP8X4), scales[:], grouped[:].rearrange("p m j -> p (m j)"))
            return codes, scales

        early_scales = gather(scale_table, U8, 0, BLOCK, "scales")
        w1_mx = quantise(w1_raw, "w1")
        w2_mx = quantise(w2_raw, "w2")

        stif_banks = [psum.tile([P, D, P], F32, name="stif_bank%d" % b) for b in range(2)]

        def product(bank, weights, words, scales):
            nc.tensor.matmul_mx(
                bank,
                lhsT=weights[0][:].bitcast(FP8X4),
                lhsT_scale=weights[1][:],
                rhs=words.bitcast(FP8X4),
                rhs_scale=scales,
                start=True,
                stop=True,
            )

        tangential = keep.tile([P, D, P], F32, name="tangential")
        normal = [keep.tile([P, D, P], F32, name="normal%d" % b) for b in range(2)]

        def spread_stiffness(b):
            for d in range(D):
                nc.tensor.transpose(stif_banks[b][:, d, :], stif_cols[:, b, d : d + 1].to_broadcast([P, P]), ident[:])

        units = []
        early_words = []
        yv_halves = psum.tile([P, 2, HALF], F32, name="yv_halves")
        for h in range(2):
            early_words.append(gather(word_table, U32, h * HALF, HALF, "words"))
            yn_half = psum.tile([P, HALF], F32, name="yn_half%d" % h)
            product(yn_half[:], w1_mx, early_words[h][:], early_scales[:, h * HALF : (h + 1) * HALF])
            grains = slice(h * P // 2, (h + 1) * P // 2)
            units.append(
                (
                    yn_half[:].rearrange("p (v d) -> p d v", d=D),
                    yv_halves[:, h, :].rearrange("p (v d) -> p d v", d=D),
                    stif_banks[0][:, :, grains],
                    (slice(None), slice(None), grains),
                )
            )
        spread_stiffness(0)
        for h in range(2):
            product(yv_halves[:, h, :], w2_mx, early_words[h][:], early_scales[:, h * HALF : (h + 1) * HALF])
        late_words = gather(word_table, U32, BLOCK, BLOCK, "words")
        late_scales = gather(scale_table, U8, BLOCK, BLOCK, "scales", tag="w2_raw")
        yn_bank = psum.tile([P, BLOCK], F32, name="yn_bank")
        yv_bank = psum.tile([P, BLOCK], F32, name="yv_bank")
        product(yn_bank[:], w1_mx, late_words[:], late_scales[:])
        product(yv_bank[:], w2_mx, late_words[:], late_scales[:])
        spread_stiffness(1)
        for h in range(2):
            pair = slice(2 * h, 2 * h + 2)
            units.append(
                (
                    yn_bank[:].rearrange("p (v d) -> p d v", d=D)[:, pair, :],
                    yv_bank[:].rearrange("p (v d) -> p d v", d=D)[:, pair, :],
                    stif_banks[1][:, pair, :],
                    (slice(None), pair, slice(None)),
                )
            )

        def fresh(name, u):
            return keep.tile(list(units[u][0].shape), F32, name="%s%d" % (name, u))

        def gap_of(u):
            gap = keep.tile(list(units[u][0].shape), F32, name="gap")
            nc.scalar.activation(gap[:], units[u][0], ACT.Abs)
            return gap

        made = []
        gap = gap_of(0)
        for u in range(len(units)):
            over, root, shifted, soft, inverse = [fresh(n, u) for n in ("over", "root", "shifted", "soft", "inverse")]
            nc.scalar.activation(over[:], gap[:], ACT.Relu, bias=rad_col[:], scale=-1.0)
            if u > 0:
                nc.scalar.activation(soft[:], gap[:], ACT.Abs_reciprocal_sqrt, bias=0.1)
            nc.scalar.activation(root[:], over[:], ACT.Abs_reciprocal_sqrt, bias=0.01)
            nc.scalar.activation(shifted[:], over[:], ACT.Square, bias=0.005)
            if u == 0:
                nc.scalar.activation(soft[:], gap[:], ACT.Abs_reciprocal_sqrt, bias=0.1)
            if u + 1 < len(units):
                gap = gap_of(u + 1)
            nc.scalar.activation(inverse[:], soft[:], ACT.Square)
            made.append((root, shifted, inverse))

        def add_turned(bank, terms, first=True, last=True):
            for i, term in enumerate(terms):
                nc.tensor.matmul(
                    bank,
                    term,
                    ident[:],
                    start=(first and i == 0),
                    stop=(last and i == len(terms) - 1),
                    is_transpose=True,
                )

        def hertz_of(u):
            hertz = fresh("hertz", u)
            root, shifted = made[u][:2]
            nc.vector.scalar_tensor_tensor(hertz[:], shifted[:], 0.005 * 0.005, root[:], ALU.subtract, ALU.mult)
            return hertz

        caps = [keep.tile([P, D, P], F32, name="cap%d" % b) for b in range(2)]
        uppers = [keep.tile([P, D, P], F32, name="upper%d" % b) for b in range(2)]
        hertz = hertz_of(0)
        for u, (yn, yv, stiff, part) in enumerate(units):
            b = u // 2
            inverse = made[u][2]
            cap, upper, slope = caps[b][part], uppers[b][part], fresh("slope", u)
            nc.vector.scalar_tensor_tensor(cap, hertz[:], 0.6, stiff, ALU.mult, ALU.mult)
            nc.vector.scalar_tensor_tensor(slope[:], yn, 1.0 / 0.6, inverse[:], ALU.mult, ALU.mult)
            nc.vector.scalar_tensor_tensor(upper, yv, 0.5, cap, ALU.mult, ALU.min)
            nc.vector.tensor_tensor(normal[b][part], slope[:], cap, ALU.mult)
            if u + 1 < len(units):
                hertz = hertz_of(u + 1)
            if b == 1:
                nc.vector.scalar_tensor_tensor(tangential[part], cap, -1.0, upper, ALU.mult, ALU.max)
                if u == 2:
                    late_sums = psum.tile([P, P], F32, name="late_sums", tag="stif_bank0")
                members = (2 * (u - 2), 2 * (u - 2) + 1)
                terms = [term[:, d, :] for term in (normal[1], tangential) for d in members]
                add_turned(late_sums[:], terms, first=(u == 2), last=(u == 3))
            if u == 1:
                lifted = psum.tile([P, D, P], F32, name="lifted", tag="yn_half0")
                for d in range(D):
                    add_turned(lifted[:, d, :], [uppers[0][:, d, :], caps[0][:, d, :]])
                early_sums = psum.tile([P, 2, P], F32, name="early_sums")
                add_turned(early_sums[:, 0, :], [term[:, d, :] for term in (uppers[0], normal[0]) for d in range(D)])
                clipped = keep.tile([P, D, P], F32, name="clipped")
                nc.scalar.activation(clipped[:], lifted[:], ACT.Relu, scale=-1.0)
                turned = keep.tile([P, P], F32, name="turned0")
                nc.scalar.copy(turned[:], early_sums[:, 0, :])
                add_turned(early_sums[:, 1, :], [turned[:]] + [clipped[:, d, :] for d in range(D)])
                result = keep.tile([P, P], F32, name="result0")
                nc.scalar.copy(result[:], early_sums[:, 1, :])
                nc.sync.dma_start(out[:, 0:P], result[:])

        turned = keep.tile([P, P], F32, name="turned1", align_bytes=64)
        nc.vector.transpose(turned[:], late_sums[:])
        rows = out.rearrange("(g i) v -> i g v", i=32)
        for a in range(4):
            queue = nc.sync if a % 2 == 0 else nc.scalar
            queue.dma_start(
                rows[:, :, P + 32 * a : P + 32 * (a + 1)],
                turned[32 * a : 32 * (a + 1), :].rearrange("p (g j) -> p g j", j=32),
            )
